import numpy as np
import ml_dtypes


def mxq(x, axis, fmt="e4m3"):
    dtype, down = {"e4m3": (ml_dtypes.float8_e4m3fn, 7), "e5m2": (ml_dtypes.float8_e5m2, 14)}[fmt]
    v = np.moveaxis(np.asarray(x, np.float32).astype(ml_dtypes.bfloat16).astype(np.float64), axis, -1)
    blocks = v.reshape(v.shape[:-1] + (-1, 32))
    amax = np.abs(blocks).max(-1, keepdims=True)
    byte = np.maximum(np.where(amax > 0, np.frexp(amax)[1] - 1 + 127, 0) - down, 1)
    scale = np.exp2(byte - 127.0)
    codes = (blocks / scale).astype(np.float32).astype(dtype).astype(np.float64)
    return np.moveaxis((codes * scale).reshape(v.shape), -1, axis)


WIDE = False


def mx_kscale(k):
    if not WIDE:
        return np.ones(k)
    levels = np.array([10, -10, 5, -5, 0])
    if k % 512:
        return np.exp2(np.random.permutation(np.resize(levels, k // 32))).repeat(32)
    a = np.empty((k // 512, 16))
    for p in range(k // 512):
        a[p, :8] = np.random.permutation(np.resize(levels, 8))
        for g in range(8):
            far = levels[np.abs(levels - a[p, g]) >= 10]
            a[p, g + 8] = far[np.random.randint(len(far))]
    return np.exp2(a.ravel()).repeat(32)


def f64(x):
    return np.asarray(x).astype(np.float64)


def striped(idx):
    return np.tile(idx.reshape(-1, 16).T, (8, 1)).astype(np.uint16)


def unstriped(offs):
    return offs[:16].T.reshape(-1).astype(np.int64)


E2M1 = np.array([0.0, 0.5, 1.0, 1.5, 2.0, 3.0, 4.0, 6.0, -0.0, -0.5, -1.0, -1.5, -2.0, -3.0, -4.0, -6.0])


def pack_weight(w, fmt):
    k, n = w.shape
    w = f64(np.asarray(w, np.float32).astype(ml_dtypes.bfloat16)).reshape(k // 32, 32, n)
    amax = np.abs(w).max(1)
    if fmt == "e4m3":
        byte = np.frexp(amax)[1] - 1 + 127 - 7
    else:
        mant, ex = np.frexp(amax / 6.0)
        byte = np.where(mant > 0.5, ex, ex - 1) + 127
    byte = np.clip(np.where(amax > 0, byte, 1), 1, 254)
    scaled = (w * np.exp2(127.0 - byte)[:, None, :]).reshape(k, n).astype(np.float32)
    by_word = np.ascontiguousarray(scaled.reshape(k // 512, 128, 4, n).transpose(0, 1, 3, 2))
    if fmt == "e4m3":
        words = by_word.astype(ml_dtypes.float8_e4m3fn).view(np.uint8)
    else:
        c = by_word.astype(ml_dtypes.float4_e2m1fn).view(np.uint8) & 0xF
        words = (c[..., 0::2] | (c[..., 1::2] << 4)).reshape(k // 512, 128, 2 * n)
    return np.ascontiguousarray(words), np.ascontiguousarray(byte.astype(np.uint8).reshape(k // 512, 16, n))


def unpack_weight(words, scales, fmt):
    g, _, n = scales.shape
    words = np.ascontiguousarray(words).reshape(g, 128, n, -1)
    if fmt == "e4m3":
        vals = words.view(ml_dtypes.float8_e4m3fn).astype(np.float64)
    else:
        nib = np.empty((g, 128, n, 4), np.uint8)
        nib[..., 0::2] = words & 0xF
        nib[..., 1::2] = words >> 4
        vals = E2M1[nib]
    vals = vals * np.repeat(np.exp2(scales.astype(np.float64) - 127.0), 8, axis=1)[..., None]
    return vals.transpose(0, 1, 3, 2).reshape(g * 512, n)


def gelu(v):
    return 0.5 * v * (1.0 + np.tanh(np.sqrt(2.0 / np.pi) * (v + 0.044715 * v**3)))


K, H, T, S, T2 = 1024, 512, 4096, 1024, 2048

def setup_inputs():
    n = np.random.standard_normal
    s = mx_kscale(K)[:, None]
    u = mx_kscale(H)[:, None]
    tab_words, tab_scales = pack_weight(n((K, T)) * s, "e4m3")
    wb4_words, wb4_scales = pack_weight(1.4 * n((K, H)) / np.sqrt(K) / s, "e2m1")
    return {
        "tab_words": tab_words,
        "tab_scales": tab_scales,
        "offs": striped(np.random.permutation(T)[:S]),
        "offs2": striped(np.random.permutation(T)[:S]),
        "offs3": striped(np.random.permutation(T2)[:S]),
        "wa": (1.4 * n((K, H)) / np.sqrt(K) / s).astype(np.float32),
        "wb4_words": wb4_words,
        "wb4_scales": wb4_scales,
        "gain": (np.exp(0.3 * n(H)) * u[:, 0]).astype(np.float32),
        "wc": (1.8 * n((H, H)) / np.sqrt(H) / u * u.T).astype(np.float32),
        "d": (np.exp(0.3 * n(H)) * u[:, 0]).astype(np.float32),
        "wgo": np.exp(0.3 * n((128, S))).astype(np.float32),
    }

def reference(tab_words, tab_scales, offs, offs2, offs3, wa, wb4_words, wb4_scales, gain, wc, d, wgo):
    TW = unpack_weight(tab_words, tab_scales, "e4m3")
    v = TW[:, unstriped(offs)]
    v2 = TW[:, unstriped(offs2)]
    wb = unpack_weight(wb4_words, wb4_scales, "e2m1")
    ga = mxq(f64(wa), 0, "e4m3").T @ v
    sb = wb.T @ v2
    z = f64(gain)[:, None] * np.minimum(ga, sb)
    y0 = mxq(f64(wc), 0, "e4m3").T @ mxq(z, 0, "e4m3")
    y = np.tanh(y0 / (f64(d)[:, None] + np.abs(z)))
    out = np.zeros((H, T2))
    out[:, unstriped(offs3)] = np.tile(f64(wgo), (H // 128, 1)) * y
    return out

@@ -1,0 +1,285 @@
+from contextlib import ExitStack
+
+import concourse.mybir as mybir
+
+K, H, T, S, T2 = 1024, 512, 4096, 1024, 2048
+FLOPS = 2 * (2 * K * H * S) + 2 * H * H * S
+
+F32 = mybir.dt.float32
+BF16 = mybir.dt.bfloat16
+I32 = mybir.dt.int32
+U32 = mybir.dt.uint32
+U16 = mybir.dt.uint16
+U8 = mybir.dt.uint8
+FP8X4 = mybir.dt.float8_e4m3fn_x4
+FP4X4 = mybir.dt.float4_e2m1fn_x4
+ACT = mybir.ActivationFunctionType
+ALU = mybir.AluOpType
+
+P = 128
+PACK = 4
+PASSES = K // (P * PACK)
+QUADS = 4
+QUAD = P // QUADS
+HALF = 512
+HALVES = S // HALF
+LIST_COLS = HALF // 16
+
+
+def tile_list_trunked_grant_rows_kernel(
+    tc, tab_words, tab_scales, offs, offs2, offs3, wa, wb4_words, wb4_scales, gain, wc, d, wgo, out
+):
+    nc = tc.nc
+    with ExitStack() as ctx:
+        keep = ctx.enter_context(tc.tile_pool(name="keep", bufs=1))
+        psum = ctx.enter_context(tc.psum_pool(name="psum", bufs=1))
+
+        def sb(name, shape, dtype, tag=""):
+            return keep.tile(shape, dtype, name=name, tag=tag, align_bytes=64)
+
+        def bank(b, name):
+            return psum.tile([P, HALF], F32, name=name, tag="bank%d" % b)
+
+        list_g = keep.tile([P, S // 16], U16, name="list_g")
+        list_s = keep.tile([P, S // 16], U16, name="list_s")
+        list_o = keep.tile([P, S // 16], U16, name="list_o")
+        tab_w = [sb("tab_w%d" % a, [P, T], I32) for a in range(PASSES)]
+        tab_s = sb("tab_s", [P, T], U8)
+        wb_w_raw = sb("wb_w_raw", [P, PASSES, H], U16)
+        wb_s_raw = sb("wb_s_raw", [P, PASSES, H], U8)
+        wb_w = sb("wb_w", [P, PASSES, H], U16)
+        wb_s = sb("wb_s", [P, PASSES, H], U8)
+        site_s1 = sb("site_s1", [P, S], U8)
+        pages = [sb("page%d" % t, [P, T2], F32) for t in range(PACK)]
+
+        nc.vector.memset(tab_s[:].bitcast(I32), 0)
+        nc.vector.memset(wb_s_raw[:].rearrange("p a c -> p (a c)").bitcast(I32), 0)
+        nc.vector.memset(site_s1[:].bitcast(I32), 0)
+        for t in range(PACK):
+            nc.vector.memset(pages[t][:], 0.0)
+
+        nc.sync.dma_start(list_g[:], offs)
+        nc.sync.dma_start(list_s[:], offs2)
+        for q in range(QUADS):
+            nc.scalar.dma_start(
+                tab_s[QUAD * q : QUAD * q + PACK * PASSES, :].bitcast(I32),
+                tab_scales[:, PACK * q : PACK * q + PACK, :].bitcast(I32),
+            )
+
+        def load_table(a):
+            nc.sync.dma_start(tab_w[a][:], tab_words[a].rearrange("p t i -> p (t i)").bitcast(I32))
+
+        def load_rows(name, rows, cols):
+            raw = sb(name, [P, PACK, cols.stop - cols.start], F32)
+            nc.sync.dma_start(raw[:], rows[:, cols].rearrange("(p j) c -> p j c", j=PACK))
+            return raw
+
+        load_table(0)
+        nc.sync.dma_start(
+            wb_w_raw[:].rearrange("p a c -> p (a c)").bitcast(I32).rearrange("p (a w) -> p a w", a=PASSES),
+            wb4_words.bitcast(I32).rearrange("a p w -> p a w"),
+        )
+        for q in range(QUADS):
+            nc.sync.dma_start(
+                wb_s_raw[QUAD * q : QUAD * q + PACK, :, :].bitcast(I32),
+                wb4_scales[:, PACK * q : PACK * q + PACK, :].bitcast(I32).rearrange("a r w -> r a w"),
+            )
+        wa_raw0 = load_rows("wa_raw0", wa[0 : P * PACK, :], slice(0, H))
+        load_table(1)
+        wa_raw1 = [
+            load_rows("wa_raw1%d" % c, wa[P * PACK : K, :], slice(c * H // 2, (c + 1) * H // 2)) for c in range(2)
+        ]
+        gain_t = sb("gain_t", [P, PACK], F32)
+        d_t = sb("d_t", [P, PACK], F32)
+        nc.sync.dma_start(gain_t[:], gain.rearrange("(p t) -> p t", t=PACK))
+        nc.sync.dma_start(d_t[:], d.rearrange("(p t) -> p t", t=PACK))
+        wc_raw = load_rows("wc_raw", wc, slice(0, H))
+        wgo_t = [sb("wgo_t%d" % h, [P, PACK, HALF], F32) for h in range(HALVES)]
+        wgo_dealt = wgo.rearrange("(q t) s -> q t s", t=PACK)
+        for h in range(HALVES):
+            for q in (0, 2, 1, 3):
+                nc.sync.dma_start(
+                    wgo_t[h][QUAD * q : QUAD * (q + 1), :, :], wgo_dealt[:, :, h * HALF : (h + 1) * HALF]
+                )
+            if h == 0:
+                nc.sync.dma_start(list_o[:], offs3)
+
+        def list_half(lst, h):
+            return lst[:, h * LIST_COLS : (h + 1) * LIST_COLS]
+
+        def gather_words(name, a, offsets, n):
+            words = sb(name, [P, n], U32)
+            nc.vector.tensor_copy(words[:], tab_w[a][:].bitcast(U32).indirect(offsets))
+            return words
+
+        def interleave(copy, grouped, raw, m0):
+            m = raw.shape[2] // PACK
+            copy(
+                grouped[:].rearrange("p (t m j) -> p m j t", t=PACK, j=PACK)[:, m0 : m0 + m],
+                raw[:].rearrange("p j (m t) -> p m j t", t=PACK),
+            )
+
+        def quantize(name, grouped):
+            n = grouped.shape[1] // PACK
+            codes = sb(name + "_c", [P, n], U32)
+            scales = sb(name + "_s", [P, n], U8)
+            nc.vector.quantize_mx(out=codes[:].bitcast(FP8X4), scales=scales[:], in_=grouped[:])
+            return codes, scales
+
+        def cols(t):
+            return slice(t * P, (t + 1) * P)
+
+        def site_pass(acc, t, a, words, h):
+            plane = (site_s0, site_s1)[a]
+            nc.tensor.matmul_mx(
+                out=acc[:],
+                lhsT=wb_w[:, a, cols(t)].bitcast(U8).bitcast(FP4X4),
+                lhsT_scale=wb_s[:, a, cols(t)],
+                rhs=words.bitcast(FP8X4),
+                rhs_scale=plane[:, h * HALF : (h + 1) * HALF],
+                start=(a == 0),
+                stop=(a == PASSES - 1),
+            )
+
+        def group_pass(acc, t, a, words, h):
+            codes, scales = wa_q[a]
+            nc.tensor.matmul_mx(
+                out=acc[:],
+                lhsT=codes[:, cols(t)].bitcast(FP8X4),
+                lhsT_scale=scales[:, cols(t)],
+                rhs=words.bitcast(FP8X4),
+                rhs_scale=group_s[PACK * a : P, h * HALF : (h + 1) * HALF],
+                start=(a == 0),
+                stop=(a == PASSES - 1),
+            )
+
+        site_s0 = sb("site_s0", [P, S], U8)
+        group_s = sb("group_s", [P, S], U8)
+        nc.vector.tensor_copy(site_s0[:], tab_s[:].indirect(list_s[:]))
+        nc.vector.tensor_copy(group_s[:], tab_s[:].indirect(list_g[:]))
+        live = 3 * QUAD + PACK
+        nc.scalar.dma_start(site_s1[0:live, :].bitcast(I32), site_s0[PACK : PACK + live, :].bitcast(I32))
+
+        nc.vector.tensor_copy(
+            wb_w[:].rearrange("p a (t m) -> p a m t", t=PACK), wb_w_raw[:].rearrange("p a (m t) -> p a m t", t=PACK)
+        )
+        nc.vector.tensor_copy(
+            wb_s[:].rearrange("p a (t m) -> p a t m", t=PACK), wb_s_raw[:].rearrange("p a (m t) -> p a t m", t=PACK)
+        )
+
+        site_w0 = gather_words("site_w0", 0, list_s[:], S)
+        group_w0 = gather_words("group_w0", 0, list_g[:], S)
+
+        wa_bf = [sb("wa_bf%d" % a, [P, PACK * H], BF16) for a in range(PASSES)]
+        interleave(nc.scalar.copy, wa_bf[0], wa_raw0, 0)
+        wa_q = [quantize("wa_q0", wa_bf[0])]
+
+        site_acc = [bank(t, "site0%d" % t) for t in range(PACK)]
+        group_acc = [bank(PACK + t, "group0%d" % t) for t in range(PACK)]
+        for t in range(PACK):
+            site_pass(site_acc[t], t, 0, site_w0[:, 0:HALF], 0)
+        for t in range(PACK):
+            group_pass(group_acc[t], t, 0, group_w0[:, 0:HALF], 0)
+
+        site_w1 = gather_words("site_w10", 1, list_half(list_s, 0), HALF)
+        group_w1 = gather_words("group_w10", 1, list_half(list_g, 0), HALF)
+        low = [sb("low%d" % h, [P, PACK, HALF], F32) for h in range(HALVES)]
+        for t in range(PACK):
+            site_pass(site_acc[t], t, 1, site_w1[:], 0)
+            nc.scalar.copy(low[0][:, t, :], site_acc[t][:])
+
+        interleave(nc.scalar.copy, wa_bf[1], wa_raw1[0], 0)
+        interleave(nc.vector.tensor_copy, wa_bf[1], wa_raw1[1], P // 2)
+        wa_q.append(quantize("wa_q1", wa_bf[1]))
+        for t in range(PACK):
+            group_pass(group_acc[t], t, 1, group_w1[:], 0)
+
+        site_w1 = gather_words("site_w11", 1, list_half(list_s, 1), HALF)
+        site_acc = [bank(t, "site1%d" % t) for t in range(PACK)]
+        for t in range(PACK):
+            site_pass(site_acc[t], t, 0, site_w0[:, HALF:S], 1)
+            site_pass(site_acc[t], t, 1, site_w1[:], 1)
+            nc.scalar.copy(low[1][:, t, :], site_acc[t][:])
+
+        for t in range(PACK):
+            nc.vector.tensor_tensor(low[0][:, t, :], group_acc[t][:], low[0][:, t, :], ALU.min)
+
+        z_bf = [sb("z_bf%d" % h, [P, PACK * HALF], BF16) for h in range(HALVES)]
+        nc.vector.tensor_tensor(
+            z_bf[0][:].rearrange("p (c i t) -> p c t i", i=PACK, t=PACK),
+            low[0][:].rearrange("p t (c i) -> p c t i", i=PACK),
+            gain_t[:].unsqueeze(1).unsqueeze(3).to_broadcast([P, HALF // PACK, PACK, PACK]),
+            ALU.mult,
+        )
+        wc_bf = sb("wc_bf", [P, PACK * H], BF16)
+        interleave(nc.scalar.copy, wc_bf, wc_raw, 0)
+        wc_c, wc_s = quantize("wc_q", wc_bf)
+
+        def mix(h, first_bank):
+            z_c, z_s = quantize("z_q%d" % h, z_bf[h])
+            accs = [bank(first_bank + t, "mix%d%d" % (h, t)) for t in range(PACK)]
+            for t in range(PACK):
+                nc.tensor.matmul_mx(
+                    out=accs[t][:],
+                    lhsT=wc_c[:, cols(t)].bitcast(FP8X4),
+                    lhsT_scale=wc_s[:, cols(t)],
+                    rhs=z_c[:].bitcast(FP8X4),
+                    rhs_scale=z_s[:],
+                    start=True,
+                    stop=True,
+                )
+            return accs
+
+        mix_acc = mix(0, PACK)
+
+        group_w1 = gather_words("group_w11", 1, list_half(list_g, 1), HALF)
+        group_acc = [bank(t, "group1%d" % t) for t in range(PACK)]
+        for t in range(PACK):
+            group_pass(group_acc[t], t, 0, group_w0[:, HALF:S], 1)
+            group_pass(group_acc[t], t, 1, group_w1[:], 1)
+
+        def size_of_z(name, tag, h):
+            size = sb(name, [P, PACK, HALF], F32, tag)
+            for t in range(PACK):
+                nc.scalar.activation(size[:, t, :], low[h][:, t, :], ACT.Abs, scale=gain_t[:, t : t + 1])
+            return size
+
+        def log_divisor(name, tag, size):
+            logs = sb(name, [P, PACK, HALF], F32, tag)
+            for t in range(PACK):
+                nc.scalar.activation(logs[:, t, :], size[:, t, :], ACT.Ln, bias=d_t[:, t : t + 1])
+            return logs
+
+        def scores(name, tag, logs, accs):
+            ratio = sb(name, [P, PACK, HALF], F32, tag)
+            for t in range(PACK):
+                nc.scalar.activation(ratio[:, t, :], logs[:, t, :], ACT.Exp, scale=-1.0)
+                nc.vector.tensor_tensor(ratio[:, t, :], accs[t][:], ratio[:, t, :], ALU.mult)
+            for t in range(PACK):
+                nc.scalar.activation(logs[:, t, :], ratio[:, t, :], ACT.Tanh)
+            return logs
+
+        def place(h, t, y):
+            nc.vector.tensor_tensor(
+                pages[t][:].indirect(list_half(list_o, h)), y[:, t, :], wgo_t[h][:, t, :], ALU.mult
+            )
+
+        y0 = scores("ratio0", "work0", log_divisor("logs0", "logs0", size_of_z("size0", "work0", 0)), mix_acc)
+
+        for t in range(PACK):
+            nc.vector.tensor_tensor(low[1][:, t, :], group_acc[t][:], low[1][:, t, :], ALU.min)
+        z1 = sb("z1", [P, PACK, HALF], F32)
+        for t in range(PACK):
+            nc.scalar.activation(z1[:, t, :], low[1][:, t, :], ACT.Copy, scale=gain_t[:, t : t + 1])
+        nc.scalar.copy(
+            z_bf[1][:].rearrange("p (c i t) -> p c t i", i=PACK, t=PACK),
+            z1[:].rearrange("p t (c i) -> p c t i", i=PACK),
+        )
+        for t in range(PACK):
+            place(0, t, y0)
+        mix_acc = mix(1, 0)
+        y1 = scores("ratio1", "work1", log_divisor("logs1", "work0", size_of_z("size1", "work1", 1)), mix_acc)
+        out_dealt = out.rearrange("(p t) c -> t p c", t=PACK)
+        for t in range(PACK):
+            place(1, t, y1)
+            nc.sync.dma_start(out_dealt[t], pages[t][:])

@@ -24,6 +24,8 @@ QUAD = P // QUADS
 HALF = 512
 HALVES = S // HALF
 LIST_COLS = HALF // 16
+SCALE_ROWS = PACK * PASSES
+SPARE = QUAD - SCALE_ROWS
 
 
 def tile_list_trunked_grant_rows_kernel(
@@ -49,20 +51,24 @@ def tile_list_trunked_grant_rows_kernel(
         wb_s_raw = sb("wb_s_raw", [P, PASSES, H], U8)
         wb_w = sb("wb_w", [P, PASSES, H], U16)
         wb_s = sb("wb_s", [P, PASSES, H], U8)
+        planes = sb("planes", [P, 2 * S], U8)
         site_s1 = sb("site_s1", [P, S], U8)
         pages = [sb("page%d" % t, [P, T2], F32) for t in range(PACK)]
 
-        nc.vector.memset(tab_s[:].bitcast(I32), 0)
-        nc.vector.memset(wb_s_raw[:].rearrange("p a c -> p (a c)").bitcast(I32), 0)
-        nc.vector.memset(site_s1[:].bitcast(I32), 0)
-        for t in range(PACK):
-            nc.vector.memset(pages[t][:], 0.0)
-
-        nc.sync.dma_start(list_g[:], offs)
-        nc.sync.dma_start(list_s[:], offs2)
+        nc.gpsimd.memset(wb_s_raw[:].rearrange("p a c -> p (a c)").bitcast(I32), 0)
         for q in range(QUADS):
-            nc.scalar.dma_start(
-                tab_s[QUAD * q : QUAD * q + PACK * PASSES, :].bitcast(I32),
+            nc.gpsimd.memset(tab_s[QUAD * q : QUAD * q + SPARE, :].bitcast(I32), 0)
+        nc.gpsimd.memset(planes[P - QUAD : P, :].bitcast(I32), 0)
+        nc.gpsimd.memset(site_s1[P - QUAD : P, :].bitcast(I32), 0)
+        for t in range(PACK):
+            for c in range(0, T2, HALF):
+                nc.gpsimd.memset(pages[t][:, c : c + HALF], 0.0)
+
+        nc.sync.dma_start(list_s[:], offs2)
+        nc.sync.dma_start(list_g[:], offs)
+        for q in range(QUADS):
+            nc.sync.dma_start(
+                tab_s[QUAD * q + SPARE : QUAD * (q + 1), :].bitcast(I32),
                 tab_scales[:, PACK * q : PACK * q + PACK, :].bitcast(I32),
             )
 
@@ -75,10 +81,7 @@ def tile_list_trunked_grant_rows_kernel(
             return raw
 
         load_table(0)
-        nc.sync.dma_start(
-            wb_w_raw[:].rearrange("p a c -> p (a c)").bitcast(I32).rearrange("p (a w) -> p a w", a=PASSES),
-            wb4_words.bitcast(I32).rearrange("a p w -> p a w"),
-        )
+        nc.sync.dma_start(wb_w_raw[:].bitcast(I32), wb4_words.bitcast(I32).rearrange("a p w -> p a w"))
         for q in range(QUADS):
             nc.sync.dma_start(
                 wb_s_raw[QUAD * q : QUAD * q + PACK, :, :].bitcast(I32),
@@ -93,7 +96,7 @@ def tile_list_trunked_grant_rows_kernel(
         d_t = sb("d_t", [P, PACK], F32)
         nc.sync.dma_start(gain_t[:], gain.rearrange("(p t) -> p t", t=PACK))
         nc.sync.dma_start(d_t[:], d.rearrange("(p t) -> p t", t=PACK))
-        wc_raw = load_rows("wc_raw", wc, slice(0, H))
+        wc_raw = [load_rows("wc_raw%d" % c, wc, slice(c * H // 2, (c + 1) * H // 2)) for c in range(2)]
         wgo_t = [sb("wgo_t%d" % h, [P, PACK, HALF], F32) for h in range(HALVES)]
         wgo_dealt = wgo.rearrange("(q t) s -> q t s", t=PACK)
         for h in range(HALVES):
@@ -130,7 +133,7 @@ def tile_list_trunked_grant_rows_kernel(
             return slice(t * P, (t + 1) * P)
 
         def site_pass(acc, t, a, words, h):
-            plane = (site_s0, site_s1)[a]
+            plane = (planes, site_s1)[a]
             nc.tensor.matmul_mx(
                 out=acc[:],
                 lhsT=wb_w[:, a, cols(t)].bitcast(U8).bitcast(FP4X4),
@@ -148,17 +151,18 @@ def tile_list_trunked_grant_rows_kernel(
                 lhsT=codes[:, cols(t)].bitcast(FP8X4),
                 lhsT_scale=scales[:, cols(t)],
                 rhs=words.bitcast(FP8X4),
-                rhs_scale=group_s[PACK * a : P, h * HALF : (h + 1) * HALF],
+                rhs_scale=planes[PACK * a : P, S + h * HALF : S + (h + 1) * HALF],
                 start=(a == 0),
                 stop=(a == PASSES - 1),
             )
 
-        site_s0 = sb("site_s0", [P, S], U8)
-        group_s = sb("group_s", [P, S], U8)
-        nc.vector.tensor_copy(site_s0[:], tab_s[:].indirect(list_s[:]))
-        nc.vector.tensor_copy(group_s[:], tab_s[:].indirect(list_g[:]))
-        live = 3 * QUAD + PACK
-        nc.scalar.dma_start(site_s1[0:live, :].bitcast(I32), site_s0[PACK : PACK + live, :].bitcast(I32))
+        picked_s = sb("picked_s", [P, 2 * S], U8)
+        nc.vector.tensor_copy(picked_s[:, 0:S], tab_s[:].indirect(list_s[:]))
+        nc.vector.tensor_copy(picked_s[:, S : 2 * S], tab_s[:].indirect(list_g[:]))
+        nc.scalar.dma_start(planes[0 : P - SPARE, :].bitcast(I32), picked_s[SPARE:P, :].bitcast(I32))
+        nc.scalar.dma_start(
+            site_s1[0 : P - SPARE - PACK, :].bitcast(I32), picked_s[SPARE + PACK : P, 0:S].bitcast(I32)
+        )
 
         nc.vector.tensor_copy(
             wb_w[:].rearrange("p a (t m) -> p a m t", t=PACK), wb_w_raw[:].rearrange("p a (m t) -> p a m t", t=PACK)
@@ -201,18 +205,24 @@ def tile_list_trunked_grant_rows_kernel(
             site_pass(site_acc[t], t, 1, site_w1[:], 1)
             nc.scalar.copy(low[1][:, t, :], site_acc[t][:])
 
-        for t in range(PACK):
-            nc.vector.tensor_tensor(low[0][:, t, :], group_acc[t][:], low[0][:, t, :], ALU.min)
+        def scaled_minimum(h):
+            z = sb("z%d" % h, [P, PACK, HALF], F32)
+            for t in range(PACK):
+                nc.vector.tensor_tensor(low[h][:, t, :], group_acc[t][:], low[h][:, t, :], ALU.min)
+                nc.gpsimd.tensor_scalar(z[:, t, :], low[h][:, t, :], gain_t[:, t : t + 1], 0.0, ALU.mult, ALU.add)
+            return z
+
+        def round_z(h, z, copy):
+            copy(
+                z_bf[h][:].rearrange("p (c i t) -> p c t i", i=PACK, t=PACK),
+                z[:].rearrange("p t (c i) -> p c t i", i=PACK),
+            )
 
         z_bf = [sb("z_bf%d" % h, [P, PACK * HALF], BF16) for h in range(HALVES)]
-        nc.vector.tensor_tensor(
-            z_bf[0][:].rearrange("p (c i t) -> p c t i", i=PACK, t=PACK),
-            low[0][:].rearrange("p t (c i) -> p c t i", i=PACK),
-            gain_t[:].unsqueeze(1).unsqueeze(3).to_broadcast([P, HALF // PACK, PACK, PACK]),
-            ALU.mult,
-        )
         wc_bf = sb("wc_bf", [P, PACK * H], BF16)
-        interleave(nc.scalar.copy, wc_bf, wc_raw, 0)
+        interleave(nc.scalar.copy, wc_bf, wc_raw[0], 0)
+        round_z(0, scaled_minimum(0), nc.vector.tensor_copy)
+        interleave(nc.vector.tensor_copy, wc_bf, wc_raw[1], P // 2)
         wc_c, wc_s = quantize("wc_q", wc_bf)
 
         def mix(h, first_bank):
@@ -250,36 +260,39 @@ def tile_list_trunked_grant_rows_kernel(
                 nc.scalar.activation(logs[:, t, :], size[:, t, :], ACT.Ln, bias=d_t[:, t : t + 1])
             return logs
 
-        def scores(name, tag, logs, accs):
-            ratio = sb(name, [P, PACK, HALF], F32, tag)
-            for t in range(PACK):
-                nc.scalar.activation(ratio[:, t, :], logs[:, t, :], ACT.Exp, scale=-1.0)
-                nc.vector.tensor_tensor(ratio[:, t, :], accs[t][:], ratio[:, t, :], ALU.mult)
-            for t in range(PACK):
-                nc.scalar.activation(logs[:, t, :], ratio[:, t, :], ACT.Tanh)
-            return logs
+        def damp(ratio, logs, accs, t):
+            nc.scalar.activation(ratio[:, t, :], logs[:, t, :], ACT.Exp, scale=-1.0)
+            nc.vector.tensor_tensor(ratio[:, t, :], accs[t][:], ratio[:, t, :], ALU.mult)
+
+        def score(y, ratio, t):
+            nc.scalar.activation(y[:, t, :], ratio[:, t, :], ACT.Tanh)
 
         def place(h, t, y):
             nc.vector.tensor_tensor(
                 pages[t][:].indirect(list_half(list_o, h)), y[:, t, :], wgo_t[h][:, t, :], ALU.mult
             )
 
-        y0 = scores("ratio0", "work0", log_divisor("logs0", "logs0", size_of_z("size0", "work0", 0)), mix_acc)
-
-        for t in range(PACK):
-            nc.vector.tensor_tensor(low[1][:, t, :], group_acc[t][:], low[1][:, t, :], ALU.min)
-        z1 = sb("z1", [P, PACK, HALF], F32)
-        for t in range(PACK):
-            nc.scalar.activation(z1[:, t, :], low[1][:, t, :], ACT.Copy, scale=gain_t[:, t : t + 1])
-        nc.scalar.copy(
-            z_bf[1][:].rearrange("p (c i t) -> p c t i", i=PACK, t=PACK),
-            z1[:].rearrange("p t (c i) -> p c t i", i=PACK),
-        )
-        for t in range(PACK):
-            place(0, t, y0)
+        z1 = scaled_minimum(1)
+        logs = log_divisor("logs0", "logs0", size_of_z("size0", "work0", 0))
+        ratio = sb("ratio0", [P, PACK, HALF], F32, "work0")
+        damp(ratio, logs, mix_acc, 0)
+        damp(ratio, logs, mix_acc, 1)
+        score(logs, ratio, 0)
+        place(0, 0, logs)
+        damp(ratio, logs, mix_acc, 2)
+        damp(ratio, logs, mix_acc, 3)
+        round_z(1, z1, nc.scalar.copy)
         mix_acc = mix(1, 0)
-        y1 = scores("ratio1", "work1", log_divisor("logs1", "work0", size_of_z("size1", "work1", 1)), mix_acc)
+        for t in range(1, PACK):
+            score(logs, ratio, t)
+            place(0, t, logs)
+
+        logs = log_divisor("logs1", "work0", size_of_z("size1", "work1", 1))
+        ratio = sb("ratio1", [P, PACK, HALF], F32, "work1")
+        for t in range(PACK):
+            damp(ratio, logs, mix_acc, t)
         out_dealt = out.rearrange("(p t) c -> t p c", t=PACK)
         for t in range(PACK):
-            place(1, t, y1)
+            score(logs, ratio, t)
+            place(1, t, logs)
             nc.sync.dma_start(out_dealt[t], pages[t][:])

@@ -75,9 +75,9 @@ def tile_list_trunked_grant_rows_kernel(
         def load_table(a):
             nc.sync.dma_start(tab_w[a][:], tab_words[a].rearrange("p t i -> p (t i)").bitcast(I32))
 
-        def load_rows(name, rows, cols):
-            raw = sb(name, [P, PACK, cols.stop - cols.start], F32)
-            nc.sync.dma_start(raw[:], rows[:, cols].rearrange("(p j) c -> p j c", j=PACK))
+        def load_rows(name, rows):
+            raw = sb(name, [P, PACK, H], F32, name)
+            nc.sync.dma_start(raw[:], rows.rearrange("(p j) c -> p j c", j=PACK))
             return raw
 
         load_table(0)
@@ -87,16 +87,13 @@ def tile_list_trunked_grant_rows_kernel(
                 wb_s_raw[QUAD * q : QUAD * q + PACK, :, :].bitcast(I32),
                 wb4_scales[:, PACK * q : PACK * q + PACK, :].bitcast(I32).rearrange("a r w -> r a w"),
             )
-        wa_raw0 = load_rows("wa_raw0", wa[0 : P * PACK, :], slice(0, H))
         load_table(1)
-        wa_raw1 = [
-            load_rows("wa_raw1%d" % c, wa[P * PACK : K, :], slice(c * H // 2, (c + 1) * H // 2)) for c in range(2)
-        ]
+        wa_raw = [load_rows("wa_raw%d" % a, wa[a * P * PACK : (a + 1) * P * PACK, :]) for a in range(PASSES)]
         gain_t = sb("gain_t", [P, PACK], F32)
         d_t = sb("d_t", [P, PACK], F32)
         nc.sync.dma_start(gain_t[:], gain.rearrange("(p t) -> p t", t=PACK))
         nc.sync.dma_start(d_t[:], d.rearrange("(p t) -> p t", t=PACK))
-        wc_raw = [load_rows("wc_raw%d" % c, wc, slice(c * H // 2, (c + 1) * H // 2)) for c in range(2)]
+        wc_raw = load_rows("wc_raw", wc)
         wgo_t = [sb("wgo_t%d" % h, [P, PACK, HALF], F32) for h in range(HALVES)]
         wgo_dealt = wgo.rearrange("(q t) s -> q t s", t=PACK)
         for h in range(HALVES):
@@ -110,15 +107,14 @@ def tile_list_trunked_grant_rows_kernel(
         def list_half(lst, h):
             return lst[:, h * LIST_COLS : (h + 1) * LIST_COLS]
 
-        def gather_words(name, a, offsets, n):
-            words = sb(name, [P, n], U32)
-            nc.vector.tensor_copy(words[:], tab_w[a][:].bitcast(U32).indirect(offsets))
+        def gather_words(name, a, lst):
+            words = sb(name, [P, S], U32)
+            nc.vector.tensor_copy(words[:], tab_w[a][:].bitcast(U32).indirect(lst[:]))
             return words
 
-        def interleave(copy, grouped, raw, m0):
-            m = raw.shape[2] // PACK
+        def interleave(copy, grouped, raw):
             copy(
-                grouped[:].rearrange("p (t m j) -> p m j t", t=PACK, j=PACK)[:, m0 : m0 + m],
+                grouped[:].rearrange("p (t m j) -> p m j t", t=PACK, j=PACK),
                 raw[:].rearrange("p j (m t) -> p m j t", t=PACK),
             )
 
@@ -132,25 +128,25 @@ def tile_list_trunked_grant_rows_kernel(
         def cols(t):
             return slice(t * P, (t + 1) * P)
 
-        def site_pass(acc, t, a, words, h):
+        def site_pass(acc, t, a, h):
             plane = (planes, site_s1)[a]
             nc.tensor.matmul_mx(
                 out=acc[:],
                 lhsT=wb_w[:, a, cols(t)].bitcast(U8).bitcast(FP4X4),
                 lhsT_scale=wb_s[:, a, cols(t)],
-                rhs=words.bitcast(FP8X4),
+                rhs=site_w[a][:, h * HALF : (h + 1) * HALF].bitcast(FP8X4),
                 rhs_scale=plane[:, h * HALF : (h + 1) * HALF],
                 start=(a == 0),
                 stop=(a == PASSES - 1),
             )
 
-        def group_pass(acc, t, a, words, h):
+        def group_pass(acc, t, a, h):
             codes, scales = wa_q[a]
             nc.tensor.matmul_mx(
                 out=acc[:],
                 lhsT=codes[:, cols(t)].bitcast(FP8X4),
                 lhsT_scale=scales[:, cols(t)],
-                rhs=words.bitcast(FP8X4),
+                rhs=group_w[a][:, h * HALF : (h + 1) * HALF].bitcast(FP8X4),
                 rhs_scale=planes[PACK * a : P, S + h * HALF : S + (h + 1) * HALF],
                 start=(a == 0),
                 stop=(a == PASSES - 1),
@@ -171,45 +167,41 @@ def tile_list_trunked_grant_rows_kernel(
             wb_s[:].rearrange("p a (t m) -> p a t m", t=PACK), wb_s_raw[:].rearrange("p a (m t) -> p a t m", t=PACK)
         )
 
-        site_w0 = gather_words("site_w0", 0, list_s[:], S)
-        group_w0 = gather_words("group_w0", 0, list_g[:], S)
+        site_w = [gather_words("site_w0", 0, list_s)]
+        group_w = [gather_words("group_w0", 0, list_g)]
+        site_w.append(gather_words("site_w1", 1, list_s))
+        group_w.append(gather_words("group_w1", 1, list_g))
+
+        def banks(name, h):
+            return [bank(PACK * h + t, "%s%d%d" % (name, h, t)) for t in range(PACK)]
 
         wa_bf = [sb("wa_bf%d" % a, [P, PACK * H], BF16) for a in range(PASSES)]
-        interleave(nc.scalar.copy, wa_bf[0], wa_raw0, 0)
+        interleave(nc.scalar.copy, wa_bf[0], wa_raw[0])
         wa_q = [quantize("wa_q0", wa_bf[0])]
-
-        site_acc = [bank(t, "site0%d" % t) for t in range(PACK)]
-        group_acc = [bank(PACK + t, "group0%d" % t) for t in range(PACK)]
-        for t in range(PACK):
-            site_pass(site_acc[t], t, 0, site_w0[:, 0:HALF], 0)
-        for t in range(PACK):
-            group_pass(group_acc[t], t, 0, group_w0[:, 0:HALF], 0)
-
-        site_w1 = gather_words("site_w10", 1, list_half(list_s, 0), HALF)
-        group_w1 = gather_words("group_w10", 1, list_half(list_g, 0), HALF)
-        low = [sb("low%d" % h, [P, PACK, HALF], F32) for h in range(HALVES)]
-        for t in range(PACK):
-            site_pass(site_acc[t], t, 1, site_w1[:], 0)
-            nc.scalar.copy(low[0][:, t, :], site_acc[t][:])
-
-        interleave(nc.scalar.copy, wa_bf[1], wa_raw1[0], 0)
-        interleave(nc.vector.tensor_copy, wa_bf[1], wa_raw1[1], P // 2)
+        interleave(nc.vector.tensor_copy, wa_bf[1], wa_raw[1])
         wa_q.append(quantize("wa_q1", wa_bf[1]))
-        for t in range(PACK):
-            group_pass(group_acc[t], t, 1, group_w1[:], 0)
 
-        site_w1 = gather_words("site_w11", 1, list_half(list_s, 1), HALF)
-        site_acc = [bank(t, "site1%d" % t) for t in range(PACK)]
-        for t in range(PACK):
-            site_pass(site_acc[t], t, 0, site_w0[:, HALF:S], 1)
-            site_pass(site_acc[t], t, 1, site_w1[:], 1)
-            nc.scalar.copy(low[1][:, t, :], site_acc[t][:])
+        site_acc = [banks("site", h) for h in range(HALVES)]
+        low_both = sb("low", [P, HALVES, PACK, HALF], F32, "wa_raw0")
+        low = [low_both[:, h] for h in range(HALVES)]
+        for a in range(PASSES):
+            for h in range(HALVES):
+                for t in range(PACK):
+                    site_pass(site_acc[h][t], t, a, h)
+                    if a == PASSES - 1:
+                        nc.scalar.copy(low[h][:, t, :], site_acc[h][t][:])
 
-        def scaled_minimum(h):
+        group_acc = [banks("group", h) for h in range(HALVES)]
+        for h in range(HALVES):
+            for t in range(PACK):
+                for a in range(PASSES):
+                    group_pass(group_acc[h][t], t, a, h)
+
+        def scaled_minimum(h, least):
             z = sb("z%d" % h, [P, PACK, HALF], F32)
             for t in range(PACK):
-                nc.vector.tensor_tensor(low[h][:, t, :], group_acc[t][:], low[h][:, t, :], ALU.min)
-                nc.gpsimd.tensor_scalar(z[:, t, :], low[h][:, t, :], gain_t[:, t : t + 1], 0.0, ALU.mult, ALU.add)
+                nc.vector.tensor_tensor(least[:, t, :], group_acc[h][t][:], low[h][:, t, :], ALU.min)
+                nc.gpsimd.tensor_scalar(z[:, t, :], least[:, t, :], gain_t[:, t : t + 1], 0.0, ALU.mult, ALU.add)
             return z
 
         def round_z(h, z, copy):
@@ -218,16 +210,16 @@ def tile_list_trunked_grant_rows_kernel(
                 z[:].rearrange("p t (c i) -> p c t i", i=PACK),
             )
 
-        z_bf = [sb("z_bf%d" % h, [P, PACK * HALF], BF16) for h in range(HALVES)]
+        z_bf = [sb("z_bf%d" % h, [P, PACK * HALF], BF16, "z_bf%d" % h) for h in range(HALVES)]
         wc_bf = sb("wc_bf", [P, PACK * H], BF16)
-        interleave(nc.scalar.copy, wc_bf, wc_raw[0], 0)
-        round_z(0, scaled_minimum(0), nc.vector.tensor_copy)
-        interleave(nc.vector.tensor_copy, wc_bf, wc_raw[1], P // 2)
+        z0 = scaled_minimum(0, low[0])
+        interleave(nc.vector.tensor_copy, wc_bf, wc_raw)
+        round_z(0, z0, nc.vector.tensor_copy)
         wc_c, wc_s = quantize("wc_q", wc_bf)
 
-        def mix(h, first_bank):
+        def mix(h):
             z_c, z_s = quantize("z_q%d" % h, z_bf[h])
-            accs = [bank(first_bank + t, "mix%d%d" % (h, t)) for t in range(PACK)]
+            accs = banks("mix", h)
             for t in range(PACK):
                 nc.tensor.matmul_mx(
                     out=accs[t][:],
@@ -240,18 +232,12 @@ def tile_list_trunked_grant_rows_kernel(
                 )
             return accs
 
-        mix_acc = mix(0, PACK)
+        mix_acc = mix(0)
 
-        group_w1 = gather_words("group_w11", 1, list_half(list_g, 1), HALF)
-        group_acc = [bank(t, "group1%d" % t) for t in range(PACK)]
-        for t in range(PACK):
-            group_pass(group_acc[t], t, 0, group_w0[:, HALF:S], 1)
-            group_pass(group_acc[t], t, 1, group_w1[:], 1)
-
-        def size_of_z(name, tag, h):
+        def size_of_z(name, tag, least):
             size = sb(name, [P, PACK, HALF], F32, tag)
             for t in range(PACK):
-                nc.scalar.activation(size[:, t, :], low[h][:, t, :], ACT.Abs, scale=gain_t[:, t : t + 1])
+                nc.scalar.activation(size[:, t, :], least[:, t, :], ACT.Abs, scale=gain_t[:, t : t + 1])
             return size
 
         def log_divisor(name, tag, size):
@@ -272,22 +258,23 @@ def tile_list_trunked_grant_rows_kernel(
                 pages[t][:].indirect(list_half(list_o, h)), y[:, t, :], wgo_t[h][:, t, :], ALU.mult
             )
 
-        z1 = scaled_minimum(1)
-        logs = log_divisor("logs0", "logs0", size_of_z("size0", "work0", 0))
+        logs = log_divisor("logs0", "logs0", size_of_z("size0", "work0", low[0]))
         ratio = sb("ratio0", [P, PACK, HALF], F32, "work0")
         damp(ratio, logs, mix_acc, 0)
         damp(ratio, logs, mix_acc, 1)
+        least1 = sb("least1", [P, PACK, HALF], F32, "z_bf0")
+        z1 = scaled_minimum(1, least1)
         score(logs, ratio, 0)
         place(0, 0, logs)
         damp(ratio, logs, mix_acc, 2)
         damp(ratio, logs, mix_acc, 3)
         round_z(1, z1, nc.scalar.copy)
-        mix_acc = mix(1, 0)
+        mix_acc = mix(1)
         for t in range(1, PACK):
             score(logs, ratio, t)
             place(0, t, logs)
 
-        logs = log_divisor("logs1", "work0", size_of_z("size1", "work1", 1))
+        logs = log_divisor("logs1", "work0", size_of_z("size1", "work1", least1))
         ratio = sb("ratio1", [P, PACK, HALF], F32, "work1")
         for t in range(PACK):
             damp(ratio, logs, mix_acc, t)

@@ -64,6 +64,11 @@ def tile_list_trunked_grant_rows_kernel(
             for c in range(0, T2, HALF):
                 nc.gpsimd.memset(pages[t][:, c : c + HALF], 0.0)
 
+        one = sb("one", [P, 1], F32)
+        warm = sb("warm", [P, 1], F32)
+        nc.vector.memset(one[:], 1.0)
+        nc.scalar.activation(warm[:], one[:], ACT.Ln)
+
         nc.sync.dma_start(list_s[:], offs2)
         nc.sync.dma_start(list_g[:], offs)
         for q in range(QUADS):

@@ -24,8 +24,9 @@ QUAD = P // QUADS
 HALF = 512
 HALVES = S // HALF
 LIST_COLS = HALF // 16
-SCALE_ROWS = PACK * PASSES
-SPARE = QUAD - SCALE_ROWS
+BLOCKS = PACK * QUADS
+SCALE_AT = P - PASSES * BLOCKS
+PAD = 8
 
 
 def tile_list_trunked_grant_rows_kernel(
@@ -45,21 +46,19 @@ def tile_list_trunked_grant_rows_kernel(
         list_g = keep.tile([P, S // 16], U16, name="list_g")
         list_s = keep.tile([P, S // 16], U16, name="list_s")
         list_o = keep.tile([P, S // 16], U16, name="list_o")
-        tab_w = [sb("tab_w%d" % a, [P, T], I32) for a in range(PASSES)]
-        tab_s = sb("tab_s", [P, T], U8)
+        tab_w = [sb("tab_w%d" % a, [P, T], I32, "tab_w%d" % a) for a in range(PASSES)]
+        tab_s = sb("tab_s", [P, T], U8, "tab_s")
         wb_w_raw = sb("wb_w_raw", [P, PASSES, H], U16)
         wb_s_raw = sb("wb_s_raw", [P, PASSES, H], U8)
         wb_w = sb("wb_w", [P, PASSES, H], U16)
         wb_s = sb("wb_s", [P, PASSES, H], U8)
-        planes = sb("planes", [P, 2 * S], U8)
-        site_s1 = sb("site_s1", [P, S], U8)
+        planes = [sb("planes%d" % a, [P, 2 * S], U8) for a in range(PASSES)]
         pages = [sb("page%d" % t, [P, T2], F32) for t in range(PACK)]
 
         nc.gpsimd.memset(wb_s_raw[:].rearrange("p a c -> p (a c)").bitcast(I32), 0)
-        for q in range(QUADS):
-            nc.gpsimd.memset(tab_s[QUAD * q : QUAD * q + SPARE, :].bitcast(I32), 0)
-        nc.gpsimd.memset(planes[P - QUAD : P, :].bitcast(I32), 0)
-        nc.gpsimd.memset(site_s1[P - QUAD : P, :].bitcast(I32), 0)
+        nc.gpsimd.memset(tab_s[0:SCALE_AT, :].bitcast(I32), 0)
+        for a in range(PASSES):
+            nc.gpsimd.memset(planes[a][:].bitcast(I32), 0)
         for t in range(PACK):
             for c in range(0, T2, HALF):
                 nc.gpsimd.memset(pages[t][:, c : c + HALF], 0.0)
@@ -70,22 +69,24 @@ def tile_list_trunked_grant_rows_kernel(
         nc.scalar.activation(warm[:], one[:], ACT.Ln)
 
         nc.sync.dma_start(list_s[:], offs2)
+        nc.sync.dma_start(
+            tab_s[SCALE_AT:P, :].bitcast(I32), tab_scales.rearrange("a b t -> (a b) t").bitcast(I32)
+        )
         nc.sync.dma_start(list_g[:], offs)
-        for q in range(QUADS):
-            nc.sync.dma_start(
-                tab_s[QUAD * q + SPARE : QUAD * (q + 1), :].bitcast(I32),
-                tab_scales[:, PACK * q : PACK * q + PACK, :].bitcast(I32),
-            )
 
         def load_table(a):
             nc.sync.dma_start(tab_w[a][:], tab_words[a].rearrange("p t i -> p (t i)").bitcast(I32))
 
-        def load_rows(name, rows):
-            raw = sb(name, [P, PACK, H], F32, name)
-            nc.sync.dma_start(raw[:], rows.rearrange("(p j) c -> p j c", j=PACK))
+        def load_rows(raw, rows):
+            nc.sync.dma_start(raw, rows.rearrange("(p j) c -> p j c", j=PACK))
             return raw
 
+        def load_wa(a, tag):
+            raw = sb("wa_raw%d" % a, [P, PACK, H], F32, tag)
+            return load_rows(raw[:], wa[a * P * PACK : (a + 1) * P * PACK, :])
+
         load_table(0)
+        nc.sync.dma_start(list_o[:], offs3)
         nc.sync.dma_start(wb_w_raw[:].bitcast(I32), wb4_words.bitcast(I32).rearrange("a p w -> p a w"))
         for q in range(QUADS):
             nc.sync.dma_start(
@@ -93,21 +94,7 @@ def tile_list_trunked_grant_rows_kernel(
                 wb4_scales[:, PACK * q : PACK * q + PACK, :].bitcast(I32).rearrange("a r w -> r a w"),
             )
         load_table(1)
-        wa_raw = [load_rows("wa_raw%d" % a, wa[a * P * PACK : (a + 1) * P * PACK, :]) for a in range(PASSES)]
-        gain_t = sb("gain_t", [P, PACK], F32)
-        d_t = sb("d_t", [P, PACK], F32)
-        nc.sync.dma_start(gain_t[:], gain.rearrange("(p t) -> p t", t=PACK))
-        nc.sync.dma_start(d_t[:], d.rearrange("(p t) -> p t", t=PACK))
-        wc_raw = load_rows("wc_raw", wc)
-        wgo_t = [sb("wgo_t%d" % h, [P, PACK, HALF], F32) for h in range(HALVES)]
-        wgo_dealt = wgo.rearrange("(q t) s -> q t s", t=PACK)
-        for h in range(HALVES):
-            for q in (0, 2, 1, 3):
-                nc.sync.dma_start(
-                    wgo_t[h][QUAD * q : QUAD * (q + 1), :, :], wgo_dealt[:, :, h * HALF : (h + 1) * HALF]
-                )
-            if h == 0:
-                nc.sync.dma_start(list_o[:], offs3)
+        wa_raw = [load_wa(0, "wa_raw0")]
 
         def list_half(lst, h):
             return lst[:, h * LIST_COLS : (h + 1) * LIST_COLS]
@@ -120,7 +107,7 @@ def tile_list_trunked_grant_rows_kernel(
         def interleave(copy, grouped, raw):
             copy(
                 grouped[:].rearrange("p (t m j) -> p m j t", t=PACK, j=PACK),
-                raw[:].rearrange("p j (m t) -> p m j t", t=PACK),
+                raw.rearrange("p j (m t) -> p m j t", t=PACK),
             )
 
         def quantize(name, grouped):
@@ -134,13 +121,12 @@ def tile_list_trunked_grant_rows_kernel(
             return slice(t * P, (t + 1) * P)
 
         def site_pass(acc, t, a, h):
-            plane = (planes, site_s1)[a]
             nc.tensor.matmul_mx(
                 out=acc[:],
                 lhsT=wb_w[:, a, cols(t)].bitcast(U8).bitcast(FP4X4),
                 lhsT_scale=wb_s[:, a, cols(t)],
                 rhs=site_w[a][:, h * HALF : (h + 1) * HALF].bitcast(FP8X4),
-                rhs_scale=plane[:, h * HALF : (h + 1) * HALF],
+                rhs_scale=planes[a][:, h * HALF : (h + 1) * HALF],
                 start=(a == 0),
                 stop=(a == PASSES - 1),
             )
@@ -152,7 +138,7 @@ def tile_list_trunked_grant_rows_kernel(
                 lhsT=codes[:, cols(t)].bitcast(FP8X4),
                 lhsT_scale=scales[:, cols(t)],
                 rhs=group_w[a][:, h * HALF : (h + 1) * HALF].bitcast(FP8X4),
-                rhs_scale=planes[PACK * a : P, S + h * HALF : S + (h + 1) * HALF],
+                rhs_scale=planes[a][:, S + h * HALF : S + (h + 1) * HALF],
                 start=(a == 0),
                 stop=(a == PASSES - 1),
             )
@@ -160,10 +146,17 @@ def tile_list_trunked_grant_rows_kernel(
         picked_s = sb("picked_s", [P, 2 * S], U8)
         nc.vector.tensor_copy(picked_s[:, 0:S], tab_s[:].indirect(list_s[:]))
         nc.vector.tensor_copy(picked_s[:, S : 2 * S], tab_s[:].indirect(list_g[:]))
-        nc.scalar.dma_start(planes[0 : P - SPARE, :].bitcast(I32), picked_s[SPARE:P, :].bitcast(I32))
-        nc.scalar.dma_start(
-            site_s1[0 : P - SPARE - PACK, :].bitcast(I32), picked_s[SPARE + PACK : P, 0:S].bitcast(I32)
-        )
+
+        def spread_scales(a):
+            for q in range(QUADS):
+                row = SCALE_AT + BLOCKS * a + PACK * q
+                nc.sync.dma_start(
+                    planes[a][QUAD * q : QUAD * q + PACK, :].bitcast(I32), picked_s[row : row + PACK, :].bitcast(I32)
+                )
+
+        spread_scales(0)
+        wa_raw.append(load_wa(1, "tab_s"))
+        spread_scales(1)
 
         nc.vector.tensor_copy(
             wb_w[:].rearrange("p a (t m) -> p a m t", t=PACK), wb_w_raw[:].rearrange("p a (m t) -> p a m t", t=PACK)
@@ -174,8 +167,25 @@ def tile_list_trunked_grant_rows_kernel(
 
         site_w = [gather_words("site_w0", 0, list_s)]
         group_w = [gather_words("group_w0", 0, list_g)]
+
+        after_pass0 = sb("after_pass0", [P, PACK * H + 2 * PAD], F32, "tab_w0")
+        wc_raw = load_rows(after_pass0[:, 0 : PACK * H].rearrange("p (j c) -> p j c", j=PACK), wc)
+        gain_t = after_pass0[:, PACK * H : PACK * H + PACK]
+        d_t = after_pass0[:, PACK * H + PAD : PACK * H + PAD + PACK]
+        nc.sync.dma_start(gain_t, gain.rearrange("(p t) -> p t", t=PACK))
+        nc.sync.dma_start(d_t, d.rearrange("(p t) -> p t", t=PACK))
+
         site_w.append(gather_words("site_w1", 1, list_s))
         group_w.append(gather_words("group_w1", 1, list_g))
+
+        wgo_both = sb("wgo_both", [P, HALVES, PACK, HALF], F32, "tab_w1")
+        wgo_t = [wgo_both[:, h] for h in range(HALVES)]
+        wgo_dealt = wgo.rearrange("(q t) s -> q t s", t=PACK)
+        for h in range(HALVES):
+            for q in (0, 2, 1, 3):
+                nc.sync.dma_start(
+                    wgo_both[QUAD * q : QUAD * (q + 1), h], wgo_dealt[:, :, h * HALF : (h + 1) * HALF]
+                )
 
         def banks(name, h):
             return [bank(PACK * h + t, "%s%d%d" % (name, h, t)) for t in range(PACK)]

from contextlib import ExitStack

import concourse.mybir as mybir

K, H, T, S, T2 = 1024, 512, 4096, 1024, 2048
FLOPS = 2 * (2 * K * H * S) + 2 * H * H * S

F32 = mybir.dt.float32
BF16 = mybir.dt.bfloat16
I32 = mybir.dt.int32
U32 = mybir.dt.uint32
U16 = mybir.dt.uint16
U8 = mybir.dt.uint8
FP8X4 = mybir.dt.float8_e4m3fn_x4
FP4X4 = mybir.dt.float4_e2m1fn_x4
ACT = mybir.ActivationFunctionType
ALU = mybir.AluOpType

P = 128
PACK = 4
PASSES = K // (P * PACK)
QUADS = 4
QUAD = P // QUADS
HALF = 512
HALVES = S // HALF
LIST_COLS = HALF // 16
BLOCKS = PACK * QUADS
SCALE_AT = P - PASSES * BLOCKS
PAD = 8


def tile_list_trunked_grant_rows_kernel(
    tc, tab_words, tab_scales, offs, offs2, offs3, wa, wb4_words, wb4_scales, gain, wc, d, wgo, out
):
    nc = tc.nc
    with ExitStack() as ctx:
        keep = ctx.enter_context(tc.tile_pool(name="keep", bufs=1))
        psum = ctx.enter_context(tc.psum_pool(name="psum", bufs=1))

        def sb(name, shape, dtype, tag=""):
            return keep.tile(shape, dtype, name=name, tag=tag, align_bytes=64)

        def bank(b, name):
            return psum.tile([P, HALF], F32, name=name, tag="bank%d" % b)

        list_g = keep.tile([P, S // 16], U16, name="list_g")
        list_s = keep.tile([P, S // 16], U16, name="list_s")
        list_o = keep.tile([P, S // 16], U16, name="list_o")
        tab_w = [sb("tab_w%d" % a, [P, T], I32, "tab_w%d" % a) for a in range(PASSES)]
        tab_s = sb("tab_s", [P, T], U8, "tab_s")
        wb_w_raw = sb("wb_w_raw", [P, PASSES, H], U16)
        wb_s_raw = sb("wb_s_raw", [P, PASSES, H], U8)
        wb_w = sb("wb_w", [P, PASSES, H], U16)
        wb_s = sb("wb_s", [P, PASSES, H], U8)
        planes = [sb("planes%d" % a, [P, 2 * S], U8) for a in range(PASSES)]
        pages = [sb("page%d" % t, [P, T2], F32) for t in range(PACK)]

        nc.gpsimd.memset(wb_s_raw[:].rearrange("p a c -> p (a c)").bitcast(I32), 0)
        nc.gpsimd.memset(tab_s[0:SCALE_AT, :].bitcast(I32), 0)
        for a in range(PASSES):
            nc.gpsimd.memset(planes[a][:].bitcast(I32), 0)
        for t in range(PACK):
            for c in range(0, T2, HALF):
                nc.gpsimd.memset(pages[t][:, c : c + HALF], 0.0)

        one = sb("one", [P, 1], F32)
        warm = sb("warm", [P, 1], F32)
        nc.vector.memset(one[:], 1.0)
        nc.scalar.activation(warm[:], one[:], ACT.Ln)

        nc.sync.dma_start(list_s[:], offs2)
        nc.sync.dma_start(
            tab_s[SCALE_AT:P, :].bitcast(I32), tab_scales.rearrange("a b t -> (a b) t").bitcast(I32)
        )
        nc.sync.dma_start(list_g[:], offs)

        def load_table(a):
            nc.sync.dma_start(tab_w[a][:], tab_words[a].rearrange("p t i -> p (t i)").bitcast(I32))

        def load_rows(raw, rows):
            nc.sync.dma_start(raw, rows.rearrange("(p j) c -> p j c", j=PACK))
            return raw

        def load_wa(a, tag):
            raw = sb("wa_raw%d" % a, [P, PACK, H], F32, tag)
            return load_rows(raw[:], wa[a * P * PACK : (a + 1) * P * PACK, :])

        load_table(0)
        nc.sync.dma_start(list_o[:], offs3)
        nc.sync.dma_start(wb_w_raw[:].bitcast(I32), wb4_words.bitcast(I32).rearrange("a p w -> p a w"))
        for q in range(QUADS):
            nc.sync.dma_start(
                wb_s_raw[QUAD * q : QUAD * q + PACK, :, :].bitcast(I32),
                wb4_scales[:, PACK * q : PACK * q + PACK, :].bitcast(I32).rearrange("a r w -> r a w"),
            )
        load_table(1)
        wa_raw = [load_wa(0, "wa_raw0")]

        def list_half(lst, h):
            return lst[:, h * LIST_COLS : (h + 1) * LIST_COLS]

        def gather_words(name, a, lst):
            words = sb(name, [P, S], U32)
            nc.vector.tensor_copy(words[:], tab_w[a][:].bitcast(U32).indirect(lst[:]))
            return words

        def interleave(copy, grouped, raw):
            copy(
                grouped[:].rearrange("p (t m j) -> p m j t", t=PACK, j=PACK),
                raw.rearrange("p j (m t) -> p m j t", t=PACK),
            )

        def quantize(name, grouped):
            n = grouped.shape[1] // PACK
            codes = sb(name + "_c", [P, n], U32)
            scales = sb(name + "_s", [P, n], U8)
            nc.vector.quantize_mx(out=codes[:].bitcast(FP8X4), scales=scales[:], in_=grouped[:])
            return codes, scales

        def cols(t):
            return slice(t * P, (t + 1) * P)

        def site_pass(acc, t, a, h):
            nc.tensor.matmul_mx(
                out=acc[:],
                lhsT=wb_w[:, a, cols(t)].bitcast(U8).bitcast(FP4X4),
                lhsT_scale=wb_s[:, a, cols(t)],
                rhs=site_w[a][:, h * HALF : (h + 1) * HALF].bitcast(FP8X4),
                rhs_scale=planes[a][:, h * HALF : (h + 1) * HALF],
                start=(a == 0),
                stop=(a == PASSES - 1),
            )

        def group_pass(acc, t, a, h):
            codes, scales = wa_q[a]
            nc.tensor.matmul_mx(
                out=acc[:],
                lhsT=codes[:, cols(t)].bitcast(FP8X4),
                lhsT_scale=scales[:, cols(t)],
                rhs=group_w[a][:, h * HALF : (h + 1) * HALF].bitcast(FP8X4),
                rhs_scale=planes[a][:, S + h * HALF : S + (h + 1) * HALF],
                start=(a == 0),
                stop=(a == PASSES - 1),
            )

        picked_s = sb("picked_s", [P, 2 * S], U8)
        nc.vector.tensor_copy(picked_s[:, 0:S], tab_s[:].indirect(list_s[:]))
        nc.vector.tensor_copy(picked_s[:, S : 2 * S], tab_s[:].indirect(list_g[:]))

        def spread_scales(a):
            for q in range(QUADS):
                row = SCALE_AT + BLOCKS * a + PACK * q
                nc.sync.dma_start(
                    planes[a][QUAD * q : QUAD * q + PACK, :].bitcast(I32), picked_s[row : row + PACK, :].bitcast(I32)
                )

        spread_scales(0)
        wa_raw.append(load_wa(1, "tab_s"))
        spread_scales(1)

        nc.vector.tensor_copy(
            wb_w[:].rearrange("p a (t m) -> p a m t", t=PACK), wb_w_raw[:].rearrange("p a (m t) -> p a m t", t=PACK)
        )
        nc.vector.tensor_copy(
            wb_s[:].rearrange("p a (t m) -> p a t m", t=PACK), wb_s_raw[:].rearrange("p a (m t) -> p a t m", t=PACK)
        )

        site_w = [gather_words("site_w0", 0, list_s)]
        group_w = [gather_words("group_w0", 0, list_g)]

        after_pass0 = sb("after_pass0", [P, PACK * H + 2 * PAD], F32, "tab_w0")
        wc_raw = load_rows(after_pass0[:, 0 : PACK * H].rearrange("p (j c) -> p j c", j=PACK), wc)
        gain_t = after_pass0[:, PACK * H : PACK * H + PACK]
        d_t = after_pass0[:, PACK * H + PAD : PACK * H + PAD + PACK]
        nc.sync.dma_start(gain_t, gain.rearrange("(p t) -> p t", t=PACK))
        nc.sync.dma_start(d_t, d.rearrange("(p t) -> p t", t=PACK))

        site_w.append(gather_words("site_w1", 1, list_s))
        group_w.append(gather_words("group_w1", 1, list_g))

        wgo_both = sb("wgo_both", [P, HALVES, PACK, HALF], F32, "tab_w1")
        wgo_t = [wgo_both[:, h] for h in range(HALVES)]
        wgo_dealt = wgo.rearrange("(q t) s -> q t s", t=PACK)
        for h in range(HALVES):
            for q in (0, 2, 1, 3):
                nc.sync.dma_start(
                    wgo_both[QUAD * q : QUAD * (q + 1), h], wgo_dealt[:, :, h * HALF : (h + 1) * HALF]
                )

        def banks(name, h):
            return [bank(PACK * h + t, "%s%d%d" % (name, h, t)) for t in range(PACK)]

        wa_bf = [sb("wa_bf%d" % a, [P, PACK * H], BF16) for a in range(PASSES)]
        interleave(nc.scalar.copy, wa_bf[0], wa_raw[0])
        wa_q = [quantize("wa_q0", wa_bf[0])]
        interleave(nc.vector.tensor_copy, wa_bf[1], wa_raw[1])
        wa_q.append(quantize("wa_q1", wa_bf[1]))

        site_acc = [banks("site", h) for h in range(HALVES)]
        low_both = sb("low", [P, HALVES, PACK, HALF], F32, "wa_raw0")
        low = [low_both[:, h] for h in range(HALVES)]
        for a in range(PASSES):
            for h in range(HALVES):
                for t in range(PACK):
                    site_pass(site_acc[h][t], t, a, h)
                    if a == PASSES - 1:
                        nc.scalar.copy(low[h][:, t, :], site_acc[h][t][:])

        group_acc = [banks("group", h) for h in range(HALVES)]
        for h in range(HALVES):
            for t in range(PACK):
                for a in range(PASSES):
                    group_pass(group_acc[h][t], t, a, h)

        def scaled_minimum(h, least):
            z = sb("z%d" % h, [P, PACK, HALF], F32)
            for t in range(PACK):
                nc.vector.tensor_tensor(least[:, t, :], group_acc[h][t][:], low[h][:, t, :], ALU.min)
                nc.gpsimd.tensor_scalar(z[:, t, :], least[:, t, :], gain_t[:, t : t + 1], 0.0, ALU.mult, ALU.add)
            return z

        def round_z(h, z, copy):
            copy(
                z_bf[h][:].rearrange("p (c i t) -> p c t i", i=PACK, t=PACK),
                z[:].rearrange("p t (c i) -> p c t i", i=PACK),
            )

        z_bf = [sb("z_bf%d" % h, [P, PACK * HALF], BF16, "z_bf%d" % h) for h in range(HALVES)]
        wc_bf = sb("wc_bf", [P, PACK * H], BF16)
        z0 = scaled_minimum(0, low[0])
        interleave(nc.vector.tensor_copy, wc_bf, wc_raw)
        round_z(0, z0, nc.vector.tensor_copy)
        wc_c, wc_s = quantize("wc_q", wc_bf)

        def mix(h):
            z_c, z_s = quantize("z_q%d" % h, z_bf[h])
            accs = banks("mix", h)
            for t in range(PACK):
                nc.tensor.matmul_mx(
                    out=accs[t][:],
                    lhsT=wc_c[:, cols(t)].bitcast(FP8X4),
                    lhsT_scale=wc_s[:, cols(t)],
                    rhs=z_c[:].bitcast(FP8X4),
                    rhs_scale=z_s[:],
                    start=True,
                    stop=True,
                )
            return accs

        mix_acc = mix(0)

        def size_of_z(name, tag, least):
            size = sb(name, [P, PACK, HALF], F32, tag)
            for t in range(PACK):
                nc.scalar.activation(size[:, t, :], least[:, t, :], ACT.Abs, scale=gain_t[:, t : t + 1])
            return size

        def log_divisor(name, tag, size):
            logs = sb(name, [P, PACK, HALF], F32, tag)
            for t in range(PACK):
                nc.scalar.activation(logs[:, t, :], size[:, t, :], ACT.Ln, bias=d_t[:, t : t + 1])
            return logs

        def damp(ratio, logs, accs, t):
            nc.scalar.activation(ratio[:, t, :], logs[:, t, :], ACT.Exp, scale=-1.0)
            nc.vector.tensor_tensor(ratio[:, t, :], accs[t][:], ratio[:, t, :], ALU.mult)

        def score(y, ratio, t):
            nc.scalar.activation(y[:, t, :], ratio[:, t, :], ACT.Tanh)

        def place(h, t, y):
            nc.vector.tensor_tensor(
                pages[t][:].indirect(list_half(list_o, h)), y[:, t, :], wgo_t[h][:, t, :], ALU.mult
            )

        logs = log_divisor("logs0", "logs0", size_of_z("size0", "work0", low[0]))
        ratio = sb("ratio0", [P, PACK, HALF], F32, "work0")
        damp(ratio, logs, mix_acc, 0)
        damp(ratio, logs, mix_acc, 1)
        least1 = sb("least1", [P, PACK, HALF], F32, "z_bf0")
        z1 = scaled_minimum(1, least1)
        score(logs, ratio, 0)
        place(0, 0, logs)
        damp(ratio, logs, mix_acc, 2)
        damp(ratio, logs, mix_acc, 3)
        round_z(1, z1, nc.scalar.copy)
        mix_acc = mix(1)
        for t in range(1, PACK):
            score(logs, ratio, t)
            place(0, t, logs)

        logs = log_divisor("logs1", "work0", size_of_z("size1", "work1", least1))
        ratio = sb("ratio1", [P, PACK, HALF], F32, "work1")
        for t in range(PACK):
            damp(ratio, logs, mix_acc, t)
        out_dealt = out.rearrange("(p t) c -> t p c", t=PACK)
        for t in range(PACK):
            score(logs, ratio, t)
            place(1, t, logs)
            nc.sync.dma_start(out_dealt[t], pages[t][:])
